import numpy as np
import ml_dtypes


def mxq(x, axis, fmt="e4m3"):
    dtype, down = {"e4m3": (ml_dtypes.float8_e4m3fn, 7), "e5m2": (ml_dtypes.float8_e5m2, 14)}[fmt]
    v = np.moveaxis(np.asarray(x, np.float32).astype(ml_dtypes.bfloat16).astype(np.float64), axis, -1)
    blocks = v.reshape(v.shape[:-1] + (-1, 32))
    amax = np.abs(blocks).max(-1, keepdims=True)
    byte = np.maximum(np.where(amax > 0, np.frexp(amax)[1] - 1 + 127, 0) - down, 1)
    scale = np.exp2(byte - 127.0)
    codes = (blocks / scale).astype(np.float32).astype(dtype).astype(np.float64)
    return np.moveaxis((codes * scale).reshape(v.shape), -1, axis)


WIDE = False


def mx_kscale(k):
    if not WIDE:
        return np.ones(k)
    levels = np.array([10, -10, 5, -5, 0])
    if k % 512:
        return np.exp2(np.random.permutation(np.resize(levels, k // 32))).repeat(32)
    a = np.empty((k // 512, 16))
    for p in range(k // 512):
        a[p, :8] = np.random.permutation(np.resize(levels, 8))
        for g in range(8):
            far = levels[np.abs(levels - a[p, g]) >= 10]
            a[p, g + 8] = far[np.random.randint(len(far))]
    return np.exp2(a.ravel()).repeat(32)


def f64(x):
    return np.asarray(x).astype(np.float64)


def striped(idx):
    return np.tile(idx.reshape(-1, 16).T, (8, 1)).astype(np.uint16)


def unstriped(offs):
    return offs[:16].T.reshape(-1).astype(np.int64)


E2M1 = np.array([0.0, 0.5, 1.0, 1.5, 2.0, 3.0, 4.0, 6.0, -0.0, -0.5, -1.0, -1.5, -2.0, -3.0, -4.0, -6.0])


def pack_weight(w, fmt):
    k, n = w.shape
    w = f64(np.asarray(w, np.float32).astype(ml_dtypes.bfloat16)).reshape(k // 32, 32, n)
    amax = np.abs(w).max(1)
    if fmt == "e4m3":
        byte = np.frexp(amax)[1] - 1 + 127 - 7
    else:
        mant, ex = np.frexp(amax / 6.0)
        byte = np.where(mant > 0.5, ex, ex - 1) + 127
    byte = np.clip(np.where(amax > 0, byte, 1), 1, 254)
    scaled = (w * np.exp2(127.0 - byte)[:, None, :]).reshape(k, n).astype(np.float32)
    by_word = np.ascontiguousarray(scaled.reshape(k // 512, 128, 4, n).transpose(0, 1, 3, 2))
    if fmt == "e4m3":
        words = by_word.astype(ml_dtypes.float8_e4m3fn).view(np.uint8)
    else:
        c = by_word.astype(ml_dtypes.float4_e2m1fn).view(np.uint8) & 0xF
        words = (c[..., 0::2] | (c[..., 1::2] << 4)).reshape(k // 512, 128, 2 * n)
    return np.ascontiguousarray(words), np.ascontiguousarray(byte.astype(np.uint8).reshape(k // 512, 16, n))


def unpack_weight(words, scales, fmt):
    g, _, n = scales.shape
    words = np.ascontiguousarray(words).reshape(g, 128, n, -1)
    if fmt == "e4m3":
        vals = words.view(ml_dtypes.float8_e4m3fn).astype(np.float64)
    else:
        nib = np.empty((g, 128, n, 4), np.uint8)
        nib[..., 0::2] = words & 0xF
        nib[..., 1::2] = words >> 4
        vals = E2M1[nib]
    vals = vals * np.repeat(np.exp2(scales.astype(np.float64) - 127.0), 8, axis=1)[..., None]
    return vals.transpose(0, 1, 3, 2).reshape(g * 512, n)


def gelu(v):
    return 0.5 * v * (1.0 + np.tanh(np.sqrt(2.0 / np.pi) * (v + 0.044715 * v**3)))


T, S, S2, K = 2048, 1024, 512, 1024


def setup_inputs():
    n = np.random.standard_normal
    s = mx_kscale(K)[:, None]
    d = {}
    d["tab_words"], d["tab_scales"] = pack_weight(n((K, T)) * s, "e4m3")
    d["offs"] = striped(np.random.permutation(T)[:S])
    d["offs2"] = striped(np.random.permutation(T)[:S2])
    d["wdist"] = (n((K, K)) / s / s.T / K).astype(np.float32)
    d["wskip_words"], d["wskip_scales"] = pack_weight(n((K, S2)) / s / K ** 0.5, "e2m1")
    d["wfix"] = (2.5 * n((K, S)) / s / K ** 0.5).astype(np.float32)
    return d


def reference(tab_words, tab_scales, offs, offs2, wdist, wskip_words, wskip_scales, wfix):
    TW = unpack_weight(tab_words, tab_scales, "e4m3")
    v = TW[:, unstriped(offs)]
    v2 = TW[:, unstriped(offs2)]
    h = np.abs(mxq(f64(wdist), 0, "e4m3").T @ v)
    e = v2.T @ mxq(h, 0, "e4m3")
    w4 = unpack_weight(wskip_words, wskip_scales, "e2m1")
    f = w4.T @ v
    gap = np.abs(e - f)
    y = v2.T @ mxq(f64(wfix), 0, "e4m3")
    return gap / (1.0 + np.exp(-y))

@@ -1,0 +1,302 @@
+from contextlib import ExitStack
+
+import concourse.mybir as mybir
+
+K, T, S, S2 = 1024, 2048, 1024, 512
+FLOPS = 2 * K * K * S + 3 * 2 * K * S2 * S
+
+F32 = mybir.dt.float32
+BF16 = mybir.dt.bfloat16
+I32 = mybir.dt.int32
+U32 = mybir.dt.uint32
+U16 = mybir.dt.uint16
+U8 = mybir.dt.uint8
+FP8X4 = mybir.dt.float8_e4m3fn_x4
+FP4X4 = mybir.dt.float4_e2m1fn_x4
+ACT = mybir.ActivationFunctionType
+ALU = mybir.AluOpType
+
+P = 128
+NB = 512
+AL = 64
+
+
+def tile_list_parade_filler_distinctness_kernel(
+    tc, tab_words, tab_scales, offs, offs2, wdist, wskip_words, wskip_scales, wfix, out
+):
+    nc = tc.nc
+    with ExitStack() as ctx:
+        keep = ctx.enter_context(tc.tile_pool(name="keep", bufs=1))
+        psum = ctx.enter_context(tc.psum_pool(name="psum", bufs=1))
+
+        def sb(name, shape, dtype, tag=None):
+            return keep.tile(shape, dtype, name=name, tag=tag or name, align_bytes=AL)
+
+        def ring(tag, bufs, shape, dtype):
+            return keep.tile(shape, dtype, name=tag, tag=tag, bufs=bufs, align_bytes=AL)
+
+        idx = keep.tile([P, S // 16], U16, name="idx")
+        idx2 = keep.tile([P, S2 // 16], U16, name="idx2")
+        tw = [sb("tw%d" % a, [P, T], I32) for a in range(2)]
+        ts = sb("ts", [P, T], U8)
+        ks = sb("ks", [P, 2, S2], U8)
+        kw = sb("kw", [P, 2, 2 * S2], U8)
+        vs1 = sb("vsmoved", [P, S], U8)
+        warm = sb("warm", [P, 2], F32)
+
+        nc.vector.memset(ts[:].bitcast(I32), 0)
+        nc.vector.memset(warm[:, 0:1], 0.0)
+        nc.scalar.activation(warm[:, 1:2], warm[:, 0:1], ACT.Sigmoid)
+        nc.vector.memset(ks[:].rearrange("p a c -> p (a c)").bitcast(I32), 0)
+        nc.vector.memset(vs1[:].bitcast(I32), 0)
+
+        wd_raw = {}
+        wf_raw = {}
+
+        def load_tab(a):
+            nc.sync.dma_start(tw[a][:], tab_words[a].rearrange("p n t -> p (n t)").bitcast(I32))
+
+        def load_w(store, name, w, a, c0, width):
+            raw = sb("%s_%d_%d" % (name, a, c0), [P, 4, width], F32)
+            nc.sync.dma_start(raw[:], w[NB * a : NB * (a + 1), c0 : c0 + width].rearrange("(p j) c -> p j c", j=4))
+            store[(a, c0)] = raw
+
+        nc.sync.dma_start(idx[:], offs)
+        load_tab(0)
+        for q in range(4):
+            nc.sync.dma_start(ts[32 * q : 32 * q + 8, :].bitcast(I32), tab_scales[:, 4 * q : 4 * q + 4, :].bitcast(I32))
+        load_w(wd_raw, "wd", wdist, 0, 0, 256)
+        load_w(wd_raw, "wd", wdist, 0, 256, 256)
+        load_w(wd_raw, "wd", wdist, 1, 0, 256)
+        load_w(wd_raw, "wd", wdist, 1, 256, 256)
+        nc.sync.dma_start(idx2[:], offs2)
+        load_tab(1)
+        for a in range(2):
+            for c0 in (512, 768):
+                load_w(wd_raw, "wd", wdist, a, c0, 256)
+            if a == 1:
+                nc.sync.dma_start(kw[:].bitcast(I32), wskip_words.rearrange("a p c -> p a c").bitcast(I32))
+        for q in range(4):
+            nc.sync.dma_start(
+                ks[32 * q : 32 * q + 4, :, :].bitcast(I32),
+                wskip_scales[:, 4 * q : 4 * q + 4, :].rearrange("a r c -> r a c").bitcast(I32),
+            )
+
+        vw = {}
+        vsall = sb("vsall", [P, S], U8)
+        vs = {}
+        v2w = {}
+
+        def gather_v(a, jh, parts=1):
+            vw[(a, jh)] = sb("vw%d%d" % (a, jh), [P, NB], U32)
+            w = NB // parts
+            for i in range(parts):
+                c0 = (NB * jh + w * i) // 16
+                nc.vector.tensor_copy(
+                    vw[(a, jh)][:, w * i : w * (i + 1)], tw[a][:].bitcast(U32).indirect(idx[:, c0 : c0 + w // 16])
+                )
+
+        def gather_vs(jh):
+            vs[jh] = vsall[:, NB * jh : NB * (jh + 1)]
+            nc.vector.tensor_copy(vs[jh], ts[:].indirect(idx[:, 32 * jh : 32 * (jh + 1)]))
+
+        def gather_v2(a, tag=None):
+            v2w[a] = sb("v2w%d" % a, [P, S2], U32, tag)
+            nc.vector.tensor_copy(v2w[a][:], tw[a][:].bitcast(U32).indirect(idx2[:]))
+
+
+        def quant(name, grouped):
+            codes = sb(name + "_c", [P, NB], U32)
+            scales = sb(name + "_s", [P, NB], U8)
+            nc.vector.quantize_mx(out=codes[:].bitcast(FP8X4), scales=scales[:], in_=grouped[:])
+            return codes, scales
+
+        wd_g = {}
+        wdq = {}
+
+        def cast_wd(a, b, copy):
+            g = sb("wdg%d%d" % (a, b), [P, 4 * NB], BF16)
+            gv = g[:].rearrange("p (t m j) -> p m j t", t=4, j=4)
+            for hh in range(2):
+                raw = wd_raw[(a, NB * b + 256 * hh)]
+                copy(gv[:, 64 * hh : 64 * (hh + 1), :, :], raw[:].rearrange("p j (m t) -> p m j t", t=4))
+            wd_g[(a, b)] = g
+
+        def quant_wd(a, b):
+            wdq[(a, b)] = quant("wdq%d%d" % (a, b), wd_g[(a, b)])
+
+        wf_g = {}
+        wfq = {}
+
+        def cast_wf(a, jh, copies, tag=None):
+            g = sb("wfg%d%d" % (a, jh), [P, 4 * NB], BF16, tag)
+            dst = g[:].rearrange("p (c i j) -> p c j i", i=4, j=4)
+            src = wf_raw[(a, NB * jh)][:].rearrange("p j (c i) -> p c j i", i=4)
+            w = P // len(copies)
+            for i, copy in enumerate(copies):
+                copy(dst[:, w * i : w * (i + 1)], src[:, w * i : w * (i + 1)])
+            wf_g[(a, jh)] = g
+
+        def quant_wf(a, jh):
+            wfq[(a, jh)] = quant("wfq%d%d" % (a, jh), wf_g[(a, jh)])
+
+        habs = {}
+        hq = {}
+
+        def h_stage(b, jh):
+            g = sb("habs%d%d" % (b, jh), [P, 4 * NB], BF16)
+            for n in range(4):
+                bank = psum.tile([P, 4, P], F32, name="hb", tag="bank", bufs=8)
+                cols = slice(P * n, P * (n + 1))
+                for a in range(2):
+                    codes, scales = wdq[(a, b)]
+                    for t in range(4):
+                        tc_ = slice(P * t, P * (t + 1))
+                        nc.tensor.matmul_mx(
+                            out=bank[:, t, :],
+                            lhsT=codes[:, tc_].bitcast(FP8X4),
+                            lhsT_scale=scales[:, tc_],
+                            rhs=vw[(a, jh)][:, cols].bitcast(FP8X4),
+                            rhs_scale=vsall[4 * a :, NB * jh + P * n : NB * jh + P * (n + 1)],
+                            start=(a == 0 and t == 0),
+                            stop=(a == 1 and t == 3),
+                        )
+                nc.scalar.activation(
+                    g[:, NB * n : NB * (n + 1)].rearrange("p (n t) -> p n t", t=4),
+                    bank[:].rearrange("p t n -> p n t"),
+                    ACT.Abs,
+                )
+            habs[(b, jh)] = g
+
+        hneg = {}
+
+        def negate_h(b, jh):
+            hneg[(b, jh)] = ring("hneg", 2, [P, 4 * NB], BF16)
+            nc.vector.tensor_scalar(hneg[(b, jh)][:], habs[(b, jh)][:], -1.0, None, op0=ALU.mult)
+
+        def quant_h(b, jh):
+            hq[(b, jh)] = quant("hq%d%d" % (b, jh), hneg[(b, jh)])
+
+        dbank = {}
+
+        def f_pass(a, jh, mis=range(4)):
+            for mi in mis:
+                if a == 0:
+                    dbank[(mi, jh)] = psum.tile([P, NB], F32, name="d%d" % mi, tag="bank", bufs=8)
+                plane = vs[jh] if a == 0 else vs1[:, NB * jh : NB * (jh + 1)]
+                nc.tensor.matmul_mx(
+                    out=dbank[(mi, jh)][:],
+                    lhsT=kw[:, a, 2 * P * mi : 2 * P * (mi + 1)].bitcast(FP4X4),
+                    lhsT_scale=ks[:, a, P * mi : P * (mi + 1)],
+                    rhs=vw[(a, jh)][:].bitcast(FP8X4),
+                    rhs_scale=plane,
+                    start=(a == 0),
+                    stop=False,
+                )
+
+        def v2_pass(bank, a, mi, moving, start, stop):
+            codes, scales = moving
+            cols = slice(P * mi, P * (mi + 1))
+            nc.tensor.matmul_mx(
+                out=bank[:],
+                lhsT=v2w[a][:, cols].bitcast(FP8X4),
+                lhsT_scale=v2s[4 * a :, cols],
+                rhs=codes[:].bitcast(FP8X4),
+                rhs_scale=scales[:],
+                start=start,
+                stop=stop,
+            )
+
+        def e_pass(b, jh, mis=range(4)):
+            for mi in mis:
+                v2_pass(dbank[(mi, jh)], b, mi, hq[(b, jh)], False, b == 1)
+
+        sig = {}
+
+        def y_stage(jh, mis=range(4)):
+            for mi in mis:
+                bank = psum.tile([P, NB], F32, name="yb", tag="bank", bufs=8)
+                for a in range(2):
+                    v2_pass(bank, a, mi, wfq[(a, jh)], a == 0, a == 1)
+                sig[(mi, jh)] = sb("sig%d%d" % (mi, jh), [P, NB], F32)
+                nc.scalar.activation(sig[(mi, jh)][:], bank[:], ACT.Sigmoid)
+
+        gaps = {}
+
+        def gap_stage(jh, mis=range(4)):
+            for mi in mis:
+                gaps[(mi, jh)] = ring("gap", 4, [P, NB], F32)
+                nc.scalar.activation(gaps[(mi, jh)][:], dbank[(mi, jh)][:], ACT.Abs)
+
+        def finish(jh, mis=range(4)):
+            for mi in mis:
+                gap = gaps[(mi, jh)]
+                res = sb("res%d%d" % (mi, jh), [P, NB], F32)
+                nc.vector.tensor_tensor(res[:], gap[:], sig[(mi, jh)][:], ALU.mult)
+                nc.sync.dma_start(out[P * mi : P * (mi + 1), NB * jh : NB * (jh + 1)], res[:])
+
+        def move_plane():
+            nc.sync.dma_start(vs1[0:112, :].bitcast(I32), vsall[4:116, :].bitcast(I32))
+
+        def load_wf():
+            for jh in range(2):
+                for a in range(2):
+                    load_w(wf_raw, "wf", wfix, a, NB * jh, NB)
+
+        on_s, on_v = nc.scalar.copy, nc.vector.tensor_copy
+        cast_wd(0, 0, on_s)
+        cast_wd(1, 0, on_s)
+        gather_v(0, 0)
+        gather_vs(0)
+        gather_v(0, 1)
+        gather_vs(1)
+        quant_wd(0, 0)
+        quant_wd(1, 0)
+        gather_v(1, 0, 2)
+        gather_v(1, 1)
+        gather_v2(0)
+        move_plane()
+        load_wf()
+        cast_wd(0, 1, on_s)
+        h_stage(0, 0)
+        quant_wd(0, 1)
+        cast_wd(1, 1, on_v)
+        quant_wd(1, 1)
+        h_stage(0, 1)
+        h_stage(1, 0)
+        v2s = sb("v2s", [P, S2], U8, "wdg11")
+        nc.vector.tensor_copy(v2s[:], ts[:].indirect(idx2[:]))
+        negate_h(0, 0)
+        quant_h(0, 0)
+        f_pass(0, 0)
+        f_pass(1, 0)
+        cast_wf(1, 0, [on_s])
+        h_stage(1, 1)
+        e_pass(0, 0)
+        negate_h(1, 0)
+        quant_h(1, 0)
+        gather_v2(1, "habs00")
+        e_pass(1, 0)
+        cast_wf(0, 0, [on_v], "habs10")
+        quant_wf(0, 0)
+        quant_wf(1, 0)
+        negate_h(0, 1)
+        quant_h(0, 1)
+        negate_h(1, 1)
+        quant_h(1, 1)
+        gap_stage(0)
+        y_stage(0)
+        cast_wf(0, 1, [on_v], "habs01")
+        quant_wf(0, 1)
+        cast_wf(1, 1, [on_v, on_s], "habs11")
+        quant_wf(1, 1)
+        finish(0)
+        for mi in range(4):
+            f_pass(0, 1, [mi])
+            f_pass(1, 1, [mi])
+            e_pass(0, 1, [mi])
+            e_pass(1, 1, [mi])
+            gap_stage(1, [mi])
+        for mi in range(4):
+            y_stage(1, [mi])
+            finish(1, [mi])

@@ -17,8 +17,15 @@ ACT = mybir.ActivationFunctionType
 ALU = mybir.AluOpType
 
 P = 128
-NB = 512
-AL = 64
+PACK = 4
+PASS = P * PACK
+HALF = 512
+PIECE = HALF // 2
+PER_COLUMN = 16
+QUADRANTS = 4
+BANKS = 8
+MOVED_ROWS = 112
+M_TILES = S2 // P
 
 
 def tile_list_parade_filler_distinctness_kernel(
@@ -29,274 +36,287 @@ def tile_list_parade_filler_distinctness_kernel(
         keep = ctx.enter_context(tc.tile_pool(name="keep", bufs=1))
         psum = ctx.enter_context(tc.psum_pool(name="psum", bufs=1))
 
-        def sb(name, shape, dtype, tag=None):
-            return keep.tile(shape, dtype, name=name, tag=tag or name, align_bytes=AL)
+        def sbuf(name, shape, dtype, on=None):
+            return keep.tile(shape, dtype, name=name, tag=on or name, align_bytes=64)
 
-        def ring(tag, bufs, shape, dtype):
-            return keep.tile(shape, dtype, name=tag, tag=tag, bufs=bufs, align_bytes=AL)
+        def bank(name, shape):
+            return psum.tile(shape, F32, name=name, tag="bank", bufs=BANKS)
 
-        idx = keep.tile([P, S // 16], U16, name="idx")
-        idx2 = keep.tile([P, S2 // 16], U16, name="idx2")
-        tw = [sb("tw%d" % a, [P, T], I32) for a in range(2)]
-        ts = sb("ts", [P, T], U8)
-        ks = sb("ks", [P, 2, S2], U8)
-        kw = sb("kw", [P, 2, 2 * S2], U8)
-        vs1 = sb("vsmoved", [P, S], U8)
-        warm = sb("warm", [P, 2], F32)
+        def on_scalar(dst, src):
+            nc.scalar.activation(dst, src, ACT.Copy)
 
-        nc.vector.memset(ts[:].bitcast(I32), 0)
-        nc.vector.memset(warm[:, 0:1], 0.0)
-        nc.scalar.activation(warm[:, 1:2], warm[:, 0:1], ACT.Sigmoid)
-        nc.vector.memset(ks[:].rearrange("p a c -> p (a c)").bitcast(I32), 0)
-        nc.vector.memset(vs1[:].bitcast(I32), 0)
+        def on_vector(dst, src):
+            nc.vector.tensor_copy(dst, src)
 
-        wd_raw = {}
-        wf_raw = {}
+        fillers = keep.tile([P, S // PER_COLUMN], U16, name="fillers")
+        suspects = keep.tile([P, S2 // PER_COLUMN], U16, name="suspects")
+        table_words = [sbuf("table_words%d" % a, [P, T], I32) for a in range(2)]
+        table_scales = sbuf("table_scales", [P, T], U8)
+        skip_words = sbuf("skip_words", [P, 2, 2 * S2], U8)
+        skip_scales = sbuf("skip_scales", [P, 2, S2], U8)
+        v_scales = sbuf("v_scales", [P, S], U8)
+        v_scales_pass1 = sbuf("v_scales_pass1", [P, S], U8)
+        v2_scales = sbuf("v2_scales", [P, S2], U8)
 
-        def load_tab(a):
-            nc.sync.dma_start(tw[a][:], tab_words[a].rearrange("p n t -> p (n t)").bitcast(I32))
+        nc.vector.memset(table_scales[:].bitcast(I32), 0)
+        nc.vector.memset(skip_scales[:].rearrange("p a c -> p (a c)").bitcast(I32), 0)
+        nc.vector.memset(v_scales_pass1[:].bitcast(I32), 0)
 
-        def load_w(store, name, w, a, c0, width):
-            raw = sb("%s_%d_%d" % (name, a, c0), [P, 4, width], F32)
-            nc.sync.dma_start(raw[:], w[NB * a : NB * (a + 1), c0 : c0 + width].rearrange("(p j) c -> p j c", j=4))
-            store[(a, c0)] = raw
+        raw = {}
 
-        nc.sync.dma_start(idx[:], offs)
-        load_tab(0)
-        for q in range(4):
-            nc.sync.dma_start(ts[32 * q : 32 * q + 8, :].bitcast(I32), tab_scales[:, 4 * q : 4 * q + 4, :].bitcast(I32))
-        load_w(wd_raw, "wd", wdist, 0, 0, 256)
-        load_w(wd_raw, "wd", wdist, 0, 256, 256)
-        load_w(wd_raw, "wd", wdist, 1, 0, 256)
-        load_w(wd_raw, "wd", wdist, 1, 256, 256)
-        nc.sync.dma_start(idx2[:], offs2)
-        load_tab(1)
-        for a in range(2):
-            for c0 in (512, 768):
-                load_w(wd_raw, "wd", wdist, a, c0, 256)
-            if a == 1:
-                nc.sync.dma_start(kw[:].bitcast(I32), wskip_words.rearrange("a p c -> p a c").bitcast(I32))
-        for q in range(4):
+        def load_table_words(a):
+            nc.sync.dma_start(table_words[a][:], tab_words[a].rearrange("p n i -> p (n i)").bitcast(I32))
+
+        def load_table_scales():
+            for q in range(QUADRANTS):
+                nc.sync.dma_start(
+                    table_scales[32 * q : 32 * q + 8, :].bitcast(I32), tab_scales[:, 4 * q : 4 * q + 4, :].bitcast(I32)
+                )
+
+        def load_skip_scales():
+            for q in range(QUADRANTS):
+                nc.sync.dma_start(
+                    skip_scales[32 * q : 32 * q + 4, :, :].bitcast(I32),
+                    wskip_scales[:, 4 * q : 4 * q + 4, :].rearrange("a r c -> r a c").bitcast(I32),
+                )
+
+        def load_weight(name, w, a, c):
+            raw[(name, a, c)] = sbuf("%s_raw%d%d" % (name, a, c), [P, PACK, HALF], F32)
             nc.sync.dma_start(
-                ks[32 * q : 32 * q + 4, :, :].bitcast(I32),
-                wskip_scales[:, 4 * q : 4 * q + 4, :].rearrange("a r c -> r a c").bitcast(I32),
+                raw[(name, a, c)][:],
+                w[PASS * a : PASS * (a + 1), HALF * c : HALF * (c + 1)].rearrange("(p i) c -> p i c", i=PACK),
             )
 
-        vw = {}
-        vsall = sb("vsall", [P, S], U8)
-        vs = {}
-        v2w = {}
+        v_words = {}
+        v2_words = {}
 
-        def gather_v(a, jh, parts=1):
-            vw[(a, jh)] = sb("vw%d%d" % (a, jh), [P, NB], U32)
-            w = NB // parts
-            for i in range(parts):
-                c0 = (NB * jh + w * i) // 16
-                nc.vector.tensor_copy(
-                    vw[(a, jh)][:, w * i : w * (i + 1)], tw[a][:].bitcast(U32).indirect(idx[:, c0 : c0 + w // 16])
-                )
+        def list_columns(first, count):
+            return slice(first // PER_COLUMN, (first + count) // PER_COLUMN)
 
-        def gather_vs(jh):
-            vs[jh] = vsall[:, NB * jh : NB * (jh + 1)]
-            nc.vector.tensor_copy(vs[jh], ts[:].indirect(idx[:, 32 * jh : 32 * (jh + 1)]))
+        def gather_v_words(a, jh, width=HALF):
+            v_words[(a, jh)] = sbuf("v_words%d%d" % (a, jh), [P, HALF], U32)
+            for c0 in range(0, HALF, width):
+                picks = fillers[:, list_columns(HALF * jh + c0, width)]
+                nc.vector.tensor_copy(v_words[(a, jh)][:, c0 : c0 + width], table_words[a][:].bitcast(U32).indirect(picks))
 
-        def gather_v2(a, tag=None):
-            v2w[a] = sb("v2w%d" % a, [P, S2], U32, tag)
-            nc.vector.tensor_copy(v2w[a][:], tw[a][:].bitcast(U32).indirect(idx2[:]))
+        def gather_v_scales(jh):
+            picks = fillers[:, list_columns(HALF * jh, HALF)]
+            nc.vector.tensor_copy(v_scales[:, HALF * jh : HALF * (jh + 1)], table_scales[:].indirect(picks))
 
+        def gather_v2_words(a, on=None):
+            v2_words[a] = sbuf("v2_words%d" % a, [P, S2], U32, on)
+            nc.vector.tensor_copy(v2_words[a][:], table_words[a][:].bitcast(U32).indirect(suspects[:]))
 
-        def quant(name, grouped):
-            codes = sb(name + "_c", [P, NB], U32)
-            scales = sb(name + "_s", [P, NB], U8)
-            nc.vector.quantize_mx(out=codes[:].bitcast(FP8X4), scales=scales[:], in_=grouped[:])
-            return codes, scales
+        grouped = {}
+        packed = {}
 
-        wd_g = {}
-        wdq = {}
+        def round_wdist(a, b, engines):
+            key = ("wdist", a, b)
+            grouped[key] = sbuf("wdist_bf%d%d" % (a, b), [P, PACK * HALF], BF16)
+            dst = grouped[key][:].rearrange("p (t m i) -> p m i t", t=PACK, i=PACK)
+            src = raw[key][:].rearrange("p i (m t) -> p m i t", t=PACK)
+            for n, copy in enumerate(engines):
+                part = slice(n * P // 2, (n + 1) * P // 2)
+                copy(dst[:, part], src[:, part])
 
-        def cast_wd(a, b, copy):
-            g = sb("wdg%d%d" % (a, b), [P, 4 * NB], BF16)
-            gv = g[:].rearrange("p (t m j) -> p m j t", t=4, j=4)
-            for hh in range(2):
-                raw = wd_raw[(a, NB * b + 256 * hh)]
-                copy(gv[:, 64 * hh : 64 * (hh + 1), :, :], raw[:].rearrange("p j (m t) -> p m j t", t=4))
-            wd_g[(a, b)] = g
+        def round_wfix(a, jh, copy):
+            key = ("wfix", a, jh)
+            grouped[key] = sbuf("wfix_bf%d%d" % (a, jh), [P, PACK * HALF], BF16)
+            copy(
+                grouped[key][:].rearrange("p (c u i) -> p c i u", u=4, i=PACK),
+                raw[key][:].rearrange("p i (c u) -> p c i u", u=4),
+            )
 
-        def quant_wd(a, b):
-            wdq[(a, b)] = quant("wdq%d%d" % (a, b), wd_g[(a, b)])
+        def quantise(*key):
+            name = "%s_mx%d%d" % key
+            codes = sbuf(name + "_codes", [P, HALF], U32)
+            scales = sbuf(name + "_scales", [P, HALF], U8)
+            nc.vector.quantize_mx(out=codes[:].bitcast(FP8X4), scales=scales[:], in_=grouped[key][:])
+            packed[key] = (codes, scales)
 
-        wf_g = {}
-        wfq = {}
+        h_banks = {}
+        h_abs = {}
 
-        def cast_wf(a, jh, copies, tag=None):
-            g = sb("wfg%d%d" % (a, jh), [P, 4 * NB], BF16, tag)
-            dst = g[:].rearrange("p (c i j) -> p c j i", i=4, j=4)
-            src = wf_raw[(a, NB * jh)][:].rearrange("p j (c i) -> p c j i", i=4)
-            w = P // len(copies)
-            for i, copy in enumerate(copies):
-                copy(dst[:, w * i : w * (i + 1)], src[:, w * i : w * (i + 1)])
-            wf_g[(a, jh)] = g
-
-        def quant_wf(a, jh):
-            wfq[(a, jh)] = quant("wfq%d%d" % (a, jh), wf_g[(a, jh)])
-
-        habs = {}
-        hq = {}
-
-        def h_stage(b, jh):
-            g = sb("habs%d%d" % (b, jh), [P, 4 * NB], BF16)
-            for n in range(4):
-                bank = psum.tile([P, 4, P], F32, name="hb", tag="bank", bufs=8)
-                cols = slice(P * n, P * (n + 1))
-                for a in range(2):
-                    codes, scales = wdq[(a, b)]
-                    for t in range(4):
-                        tc_ = slice(P * t, P * (t + 1))
-                        nc.tensor.matmul_mx(
-                            out=bank[:, t, :],
-                            lhsT=codes[:, tc_].bitcast(FP8X4),
-                            lhsT_scale=scales[:, tc_],
-                            rhs=vw[(a, jh)][:, cols].bitcast(FP8X4),
-                            rhs_scale=vsall[4 * a :, NB * jh + P * n : NB * jh + P * (n + 1)],
-                            start=(a == 0 and t == 0),
-                            stop=(a == 1 and t == 3),
-                        )
-                nc.scalar.activation(
-                    g[:, NB * n : NB * (n + 1)].rearrange("p (n t) -> p n t", t=4),
-                    bank[:].rearrange("p t n -> p n t"),
-                    ACT.Abs,
-                )
-            habs[(b, jh)] = g
-
-        hneg = {}
+        def h_pass(a, b, jh, numbers=range(4)):
+            codes, scales = packed[("wdist", a, b)]
+            for n in numbers:
+                c, w = divmod(n, 2)
+                if a == 0:
+                    h_banks[(b, jh, n)] = bank("h_bank", [P, 2, PIECE])
+                for u in range(2):
+                    stationary = slice(P * (2 * w + u), P * (2 * w + u + 1))
+                    j0 = HALF * jh + PIECE * c
+                    nc.tensor.matmul_mx(
+                        out=h_banks[(b, jh, n)][:, u, :],
+                        lhsT=codes[:, stationary].bitcast(FP8X4),
+                        lhsT_scale=scales[:, stationary],
+                        rhs=v_words[(a, jh)][:, PIECE * c : PIECE * (c + 1)].bitcast(FP8X4),
+                        rhs_scale=v_scales[4 * a :, j0 : j0 + PIECE],
+                        start=(a == 0 and u == 0),
+                        stop=(a == 1 and u == 1),
+                    )
+                if a == 1:
+                    first = 2 * (HALF * w + PIECE * c)
+                    nc.scalar.activation(
+                        h_abs[(b, jh)][:, first : first + 2 * PIECE].rearrange("p (j u) -> p j u", u=2),
+                        h_banks[(b, jh, n)][:].rearrange("p u j -> p j u"),
+                        ACT.Abs,
+                    )
 
         def negate_h(b, jh):
-            hneg[(b, jh)] = ring("hneg", 2, [P, 4 * NB], BF16)
-            nc.vector.tensor_scalar(hneg[(b, jh)][:], habs[(b, jh)][:], -1.0, None, op0=ALU.mult)
+            nc.vector.tensor_scalar(
+                grouped[("h", b, jh)][:].rearrange("p (j w u) -> p j w u", w=2, u=2),
+                h_abs[(b, jh)][:].rearrange("p (w j u) -> p j w u", w=2, u=2),
+                -1.0,
+                None,
+                op0=ALU.mult,
+            )
 
-        def quant_h(b, jh):
-            hq[(b, jh)] = quant("hq%d%d" % (b, jh), hneg[(b, jh)])
+        diff_banks = {}
+        tanh_y = {}
+        half_gap = {}
 
-        dbank = {}
-
-        def f_pass(a, jh, mis=range(4)):
-            for mi in mis:
-                if a == 0:
-                    dbank[(mi, jh)] = psum.tile([P, NB], F32, name="d%d" % mi, tag="bank", bufs=8)
-                plane = vs[jh] if a == 0 else vs1[:, NB * jh : NB * (jh + 1)]
-                nc.tensor.matmul_mx(
-                    out=dbank[(mi, jh)][:],
-                    lhsT=kw[:, a, 2 * P * mi : 2 * P * (mi + 1)].bitcast(FP4X4),
-                    lhsT_scale=ks[:, a, P * mi : P * (mi + 1)],
-                    rhs=vw[(a, jh)][:].bitcast(FP8X4),
-                    rhs_scale=plane,
-                    start=(a == 0),
-                    stop=False,
-                )
-
-        def v2_pass(bank, a, mi, moving, start, stop):
-            codes, scales = moving
-            cols = slice(P * mi, P * (mi + 1))
+        def f_pass(a, jh, mi):
+            if a == 0:
+                diff_banks[(mi, jh)] = bank("diff_bank", [P, HALF])
+            scales = v_scales if a == 0 else v_scales_pass1
             nc.tensor.matmul_mx(
-                out=bank[:],
-                lhsT=v2w[a][:, cols].bitcast(FP8X4),
-                lhsT_scale=v2s[4 * a :, cols],
+                out=diff_banks[(mi, jh)][:],
+                lhsT=skip_words[:, a, 2 * P * mi : 2 * P * (mi + 1)].bitcast(FP4X4),
+                lhsT_scale=skip_scales[:, a, P * mi : P * (mi + 1)],
+                rhs=v_words[(a, jh)][:].bitcast(FP8X4),
+                rhs_scale=scales[:, HALF * jh : HALF * (jh + 1)],
+                start=(a == 0),
+                stop=False,
+            )
+
+        def v2_pass(acc, a, mi, moving, start, stop):
+            codes, scales = moving
+            stationary = slice(P * mi, P * (mi + 1))
+            nc.tensor.matmul_mx(
+                out=acc[:],
+                lhsT=v2_words[a][:, stationary].bitcast(FP8X4),
+                lhsT_scale=v2_scales[4 * a :, stationary],
                 rhs=codes[:].bitcast(FP8X4),
                 rhs_scale=scales[:],
                 start=start,
                 stop=stop,
             )
 
-        def e_pass(b, jh, mis=range(4)):
-            for mi in mis:
-                v2_pass(dbank[(mi, jh)], b, mi, hq[(b, jh)], False, b == 1)
+        def e_pass(b, jh, mi):
+            v2_pass(diff_banks[(mi, jh)], b, mi, packed[("h", b, jh)], False, b == 1)
 
-        sig = {}
+        def y_tile(jh, mi):
+            acc = bank("y_bank", [P, HALF])
+            for a in range(2):
+                v2_pass(acc, a, mi, packed[("wfix", a, jh)], a == 0, a == 1)
+            tanh_y[(mi, jh)] = sbuf("tanh_y%d%d" % (mi, jh), [P, HALF], F32)
+            nc.scalar.activation(tanh_y[(mi, jh)][:], acc[:], ACT.Tanh, scale=0.5)
 
-        def y_stage(jh, mis=range(4)):
-            for mi in mis:
-                bank = psum.tile([P, NB], F32, name="yb", tag="bank", bufs=8)
-                for a in range(2):
-                    v2_pass(bank, a, mi, wfq[(a, jh)], a == 0, a == 1)
-                sig[(mi, jh)] = sb("sig%d%d" % (mi, jh), [P, NB], F32)
-                nc.scalar.activation(sig[(mi, jh)][:], bank[:], ACT.Sigmoid)
+        def gap_tile(jh, mi, cols=slice(0, HALF)):
+            nc.scalar.activation(half_gap[(mi, jh)][:, cols], diff_banks[(mi, jh)][:, cols], ACT.Abs, scale=0.5)
 
-        gaps = {}
+        def finish_tile(jh, mi, cols=slice(0, HALF)):
+            result = sbuf("result%d%d_%d" % (mi, jh, cols.start), [P, cols.stop - cols.start], F32)
+            nc.vector.scalar_tensor_tensor(
+                result[:], tanh_y[(mi, jh)][:, cols], 1.0, half_gap[(mi, jh)][:, cols], ALU.add, ALU.mult
+            )
+            nc.sync.dma_start(out[P * mi : P * (mi + 1), HALF * jh + cols.start : HALF * jh + cols.stop], result[:])
 
-        def gap_stage(jh, mis=range(4)):
-            for mi in mis:
-                gaps[(mi, jh)] = ring("gap", 4, [P, NB], F32)
-                nc.scalar.activation(gaps[(mi, jh)][:], dbank[(mi, jh)][:], ACT.Abs)
+        nc.sync.dma_start(fillers[:], offs)
+        load_table_words(0)
+        load_table_scales()
+        nc.sync.dma_start(suspects[:], offs2)
+        load_weight("wdist", wdist, 0, 0)
+        load_weight("wdist", wdist, 1, 0)
+        load_table_words(1)
+        load_weight("wdist", wdist, 0, 1)
 
-        def finish(jh, mis=range(4)):
-            for mi in mis:
-                gap = gaps[(mi, jh)]
-                res = sb("res%d%d" % (mi, jh), [P, NB], F32)
-                nc.vector.tensor_tensor(res[:], gap[:], sig[(mi, jh)][:], ALU.mult)
-                nc.sync.dma_start(out[P * mi : P * (mi + 1), NB * jh : NB * (jh + 1)], res[:])
+        round_wdist(0, 0, [on_scalar, on_scalar])
+        round_wdist(1, 0, [on_scalar, on_vector])
+        round_wdist(0, 1, [on_scalar, on_vector])
+        for jh in range(2):
+            gather_v_words(0, jh)
+            gather_v_scales(jh)
 
-        def move_plane():
-            nc.sync.dma_start(vs1[0:112, :].bitcast(I32), vsall[4:116, :].bitcast(I32))
+        load_weight("wdist", wdist, 1, 1)
+        nc.sync.dma_start(skip_words[:].bitcast(I32), wskip_words.rearrange("a p c -> p a c").bitcast(I32))
+        load_skip_scales()
+        nc.sync.dma_start(v_scales_pass1[0:MOVED_ROWS, :].bitcast(I32), v_scales[4 : 4 + MOVED_ROWS, :].bitcast(I32))
+        for jh in range(2):
+            for a in range(2):
+                load_weight("wfix", wfix, a, jh)
 
-        def load_wf():
-            for jh in range(2):
-                for a in range(2):
-                    load_w(wf_raw, "wf", wfix, a, NB * jh, NB)
+        quantise("wdist", 0, 0)
+        for jh in range(2):
+            h_pass(0, 0, jh)
+        quantise("wdist", 1, 0)
+        gather_v_words(1, 0, PIECE)
+        gather_v_words(1, 1)
+        gather_v2_words(0)
+        quantise("wdist", 0, 1)
+        round_wdist(1, 1, [on_vector, on_vector])
+        h_abs_b0 = sbuf("h_abs_b0", [P, 2 * PACK * HALF], BF16, on="wdist_raw01")
+        for jh in range(2):
+            h_abs[(0, jh)] = h_abs_b0[:, PACK * HALF * jh : PACK * HALF * (jh + 1)]
+        h_pass(1, 0, 0)
+        quantise("wdist", 1, 1)
+        h_pass(1, 0, 1)
+        nc.vector.tensor_copy(v2_scales[:], table_scales[:].indirect(suspects[:]))
 
-        on_s, on_v = nc.scalar.copy, nc.vector.tensor_copy
-        cast_wd(0, 0, on_s)
-        cast_wd(1, 0, on_s)
-        gather_v(0, 0)
-        gather_vs(0)
-        gather_v(0, 1)
-        gather_vs(1)
-        quant_wd(0, 0)
-        quant_wd(1, 0)
-        gather_v(1, 0, 2)
-        gather_v(1, 1)
-        gather_v2(0)
-        move_plane()
-        load_wf()
-        cast_wd(0, 1, on_s)
-        h_stage(0, 0)
-        quant_wd(0, 1)
-        cast_wd(1, 1, on_v)
-        quant_wd(1, 1)
-        h_stage(0, 1)
-        h_stage(1, 0)
-        v2s = sb("v2s", [P, S2], U8, "wdg11")
-        nc.vector.tensor_copy(v2s[:], ts[:].indirect(idx2[:]))
+        h_abs[(1, 0)] = sbuf("h_abs10", [P, PACK * HALF], BF16)
+        for a in range(2):
+            h_pass(a, 1, 0)
+        for a in range(2):
+            for mi in range(M_TILES):
+                f_pass(a, 0, mi)
+        h_neg_b0 = sbuf("h_neg_b0", [P, 2 * PACK * HALF], BF16, on="wdist_raw11")
+        for jh in range(2):
+            grouped[("h", 0, jh)] = h_neg_b0[:, PACK * HALF * jh : PACK * HALF * (jh + 1)]
         negate_h(0, 0)
-        quant_h(0, 0)
-        f_pass(0, 0)
-        f_pass(1, 0)
-        cast_wf(1, 0, [on_s])
-        h_stage(1, 1)
-        e_pass(0, 0)
+        quantise("h", 0, 0)
+        gather_v2_words(1, on="wdist_bf11")
+        h_abs[(1, 1)] = sbuf("h_abs11", [P, PACK * HALF], BF16, on="wfix_raw10")
+        for n in range(4):
+            for a in range(2):
+                h_pass(a, 1, 1, [n])
+        for mi in range(M_TILES):
+            e_pass(0, 0, mi)
+        grouped[("h", 1, 0)] = sbuf("h_neg10", [P, PACK * HALF], BF16)
         negate_h(1, 0)
-        quant_h(1, 0)
-        gather_v2(1, "habs00")
-        e_pass(1, 0)
-        cast_wf(0, 0, [on_v], "habs10")
-        quant_wf(0, 0)
-        quant_wf(1, 0)
-        negate_h(0, 1)
-        quant_h(0, 1)
-        negate_h(1, 1)
-        quant_h(1, 1)
-        gap_stage(0)
-        y_stage(0)
-        cast_wf(0, 1, [on_v], "habs01")
-        quant_wf(0, 1)
-        cast_wf(1, 1, [on_v, on_s], "habs11")
-        quant_wf(1, 1)
-        finish(0)
-        for mi in range(4):
-            f_pass(0, 1, [mi])
-            f_pass(1, 1, [mi])
-            e_pass(0, 1, [mi])
-            e_pass(1, 1, [mi])
-            gap_stage(1, [mi])
-        for mi in range(4):
-            y_stage(1, [mi])
-            finish(1, [mi])
+        quantise("h", 1, 0)
+        for mi in range(M_TILES):
+            e_pass(1, 0, mi)
+
+        round_wfix(0, 0, on_vector)
+        quantise("wfix", 0, 0)
+        round_wfix(1, 0, on_scalar)
+        quantise("wfix", 1, 0)
+        grouped[("h", 1, 1)] = sbuf("h_neg11", [P, PACK * HALF], BF16)
+        for b in range(2):
+            negate_h(b, 1)
+            quantise("h", b, 1)
+        for a in range(2):
+            round_wfix(a, 1, on_vector)
+            quantise("wfix", a, 1)
+
+        half_gap_j0 = sbuf("half_gap_j0", [P, M_TILES * HALF], F32, on="wfix_bf10")
+        for mi in range(M_TILES):
+            half_gap[(mi, 0)] = half_gap_j0[:, HALF * mi : HALF * (mi + 1)]
+            gap_tile(0, mi)
+        for mi in range(M_TILES):
+            y_tile(0, mi)
+        for mi in range(M_TILES):
+            finish_tile(0, mi)
+
+        for mi in range(M_TILES):
+            y_tile(1, mi)
+            for a in range(2):
+                f_pass(a, 1, mi)
+            for b in range(2):
+                e_pass(b, 1, mi)
+            half_gap[(mi, 1)] = sbuf("half_gap%d1" % mi, [P, HALF], F32)
+            width = PIECE if mi == M_TILES - 1 else HALF
+            for c0 in range(0, HALF, width):
+                gap_tile(1, mi, slice(c0, c0 + width))
+                finish_tile(1, mi, slice(c0, c0 + width))

from contextlib import ExitStack

import concourse.mybir as mybir

K, T, S, S2 = 1024, 2048, 1024, 512
FLOPS = 2 * K * K * S + 3 * 2 * K * S2 * S

F32 = mybir.dt.float32
BF16 = mybir.dt.bfloat16
I32 = mybir.dt.int32
U32 = mybir.dt.uint32
U16 = mybir.dt.uint16
U8 = mybir.dt.uint8
FP8X4 = mybir.dt.float8_e4m3fn_x4
FP4X4 = mybir.dt.float4_e2m1fn_x4
ACT = mybir.ActivationFunctionType
ALU = mybir.AluOpType

P = 128
PACK = 4
PASS = P * PACK
HALF = 512
PIECE = HALF // 2
PER_COLUMN = 16
QUADRANTS = 4
BANKS = 8
MOVED_ROWS = 112
M_TILES = S2 // P


def tile_list_parade_filler_distinctness_kernel(
    tc, tab_words, tab_scales, offs, offs2, wdist, wskip_words, wskip_scales, wfix, out
):
    nc = tc.nc
    with ExitStack() as ctx:
        keep = ctx.enter_context(tc.tile_pool(name="keep", bufs=1))
        psum = ctx.enter_context(tc.psum_pool(name="psum", bufs=1))

        def sbuf(name, shape, dtype, on=None):
            return keep.tile(shape, dtype, name=name, tag=on or name, align_bytes=64)

        def bank(name, shape):
            return psum.tile(shape, F32, name=name, tag="bank", bufs=BANKS)

        def on_scalar(dst, src):
            nc.scalar.activation(dst, src, ACT.Copy)

        def on_vector(dst, src):
            nc.vector.tensor_copy(dst, src)

        fillers = keep.tile([P, S // PER_COLUMN], U16, name="fillers")
        suspects = keep.tile([P, S2 // PER_COLUMN], U16, name="suspects")
        table_words = [sbuf("table_words%d" % a, [P, T], I32) for a in range(2)]
        table_scales = sbuf("table_scales", [P, T], U8)
        skip_words = sbuf("skip_words", [P, 2, 2 * S2], U8)
        skip_scales = sbuf("skip_scales", [P, 2, S2], U8)
        v_scales = sbuf("v_scales", [P, S], U8)
        v_scales_pass1 = sbuf("v_scales_pass1", [P, S], U8)
        v2_scales = sbuf("v2_scales", [P, S2], U8)

        nc.vector.memset(table_scales[:].bitcast(I32), 0)
        nc.vector.memset(skip_scales[:].rearrange("p a c -> p (a c)").bitcast(I32), 0)
        nc.vector.memset(v_scales_pass1[:].bitcast(I32), 0)

        raw = {}

        def load_table_words(a):
            nc.sync.dma_start(table_words[a][:], tab_words[a].rearrange("p n i -> p (n i)").bitcast(I32))

        def load_table_scales():
            for q in range(QUADRANTS):
                nc.sync.dma_start(
                    table_scales[32 * q : 32 * q + 8, :].bitcast(I32), tab_scales[:, 4 * q : 4 * q + 4, :].bitcast(I32)
                )

        def load_skip_scales():
            for q in range(QUADRANTS):
                nc.sync.dma_start(
                    skip_scales[32 * q : 32 * q + 4, :, :].bitcast(I32),
                    wskip_scales[:, 4 * q : 4 * q + 4, :].rearrange("a r c -> r a c").bitcast(I32),
                )

        def load_weight(name, w, a, c):
            raw[(name, a, c)] = sbuf("%s_raw%d%d" % (name, a, c), [P, PACK, HALF], F32)
            nc.sync.dma_start(
                raw[(name, a, c)][:],
                w[PASS * a : PASS * (a + 1), HALF * c : HALF * (c + 1)].rearrange("(p i) c -> p i c", i=PACK),
            )

        v_words = {}
        v2_words = {}

        def list_columns(first, count):
            return slice(first // PER_COLUMN, (first + count) // PER_COLUMN)

        def gather_v_words(a, jh, width=HALF):
            v_words[(a, jh)] = sbuf("v_words%d%d" % (a, jh), [P, HALF], U32)
            for c0 in range(0, HALF, width):
                picks = fillers[:, list_columns(HALF * jh + c0, width)]
                nc.vector.tensor_copy(v_words[(a, jh)][:, c0 : c0 + width], table_words[a][:].bitcast(U32).indirect(picks))

        def gather_v_scales(jh):
            picks = fillers[:, list_columns(HALF * jh, HALF)]
            nc.vector.tensor_copy(v_scales[:, HALF * jh : HALF * (jh + 1)], table_scales[:].indirect(picks))

        def gather_v2_words(a, on=None):
            v2_words[a] = sbuf("v2_words%d" % a, [P, S2], U32, on)
            nc.vector.tensor_copy(v2_words[a][:], table_words[a][:].bitcast(U32).indirect(suspects[:]))

        grouped = {}
        packed = {}

        def round_wdist(a, b, engines):
            key = ("wdist", a, b)
            grouped[key] = sbuf("wdist_bf%d%d" % (a, b), [P, PACK * HALF], BF16)
            dst = grouped[key][:].rearrange("p (t m i) -> p m i t", t=PACK, i=PACK)
            src = raw[key][:].rearrange("p i (m t) -> p m i t", t=PACK)
            for n, copy in enumerate(engines):
                part = slice(n * P // 2, (n + 1) * P // 2)
                copy(dst[:, part], src[:, part])

        def round_wfix(a, jh, copy):
            key = ("wfix", a, jh)
            grouped[key] = sbuf("wfix_bf%d%d" % (a, jh), [P, PACK * HALF], BF16)
            copy(
                grouped[key][:].rearrange("p (c u i) -> p c i u", u=4, i=PACK),
                raw[key][:].rearrange("p i (c u) -> p c i u", u=4),
            )

        def quantise(*key):
            name = "%s_mx%d%d" % key
            codes = sbuf(name + "_codes", [P, HALF], U32)
            scales = sbuf(name + "_scales", [P, HALF], U8)
            nc.vector.quantize_mx(out=codes[:].bitcast(FP8X4), scales=scales[:], in_=grouped[key][:])
            packed[key] = (codes, scales)

        h_banks = {}
        h_abs = {}

        def h_pass(a, b, jh, numbers=range(4)):
            codes, scales = packed[("wdist", a, b)]
            for n in numbers:
                c, w = divmod(n, 2)
                if a == 0:
                    h_banks[(b, jh, n)] = bank("h_bank", [P, 2, PIECE])
                for u in range(2):
                    stationary = slice(P * (2 * w + u), P * (2 * w + u + 1))
                    j0 = HALF * jh + PIECE * c
                    nc.tensor.matmul_mx(
                        out=h_banks[(b, jh, n)][:, u, :],
                        lhsT=codes[:, stationary].bitcast(FP8X4),
                        lhsT_scale=scales[:, stationary],
                        rhs=v_words[(a, jh)][:, PIECE * c : PIECE * (c + 1)].bitcast(FP8X4),
                        rhs_scale=v_scales[4 * a :, j0 : j0 + PIECE],
                        start=(a == 0 and u == 0),
                        stop=(a == 1 and u == 1),
                    )
                if a == 1:
                    first = 2 * (HALF * w + PIECE * c)
                    nc.scalar.activation(
                        h_abs[(b, jh)][:, first : first + 2 * PIECE].rearrange("p (j u) -> p j u", u=2),
                        h_banks[(b, jh, n)][:].rearrange("p u j -> p j u"),
                        ACT.Abs,
                    )

        def negate_h(b, jh):
            nc.vector.tensor_scalar(
                grouped[("h", b, jh)][:].rearrange("p (j w u) -> p j w u", w=2, u=2),
                h_abs[(b, jh)][:].rearrange("p (w j u) -> p j w u", w=2, u=2),
                -1.0,
                None,
                op0=ALU.mult,
            )

        diff_banks = {}
        tanh_y = {}
        half_gap = {}

        def f_pass(a, jh, mi):
            if a == 0:
                diff_banks[(mi, jh)] = bank("diff_bank", [P, HALF])
            scales = v_scales if a == 0 else v_scales_pass1
            nc.tensor.matmul_mx(
                out=diff_banks[(mi, jh)][:],
                lhsT=skip_words[:, a, 2 * P * mi : 2 * P * (mi + 1)].bitcast(FP4X4),
                lhsT_scale=skip_scales[:, a, P * mi : P * (mi + 1)],
                rhs=v_words[(a, jh)][:].bitcast(FP8X4),
                rhs_scale=scales[:, HALF * jh : HALF * (jh + 1)],
                start=(a == 0),
                stop=False,
            )

        def v2_pass(acc, a, mi, moving, start, stop):
            codes, scales = moving
            stationary = slice(P * mi, P * (mi + 1))
            nc.tensor.matmul_mx(
                out=acc[:],
                lhsT=v2_words[a][:, stationary].bitcast(FP8X4),
                lhsT_scale=v2_scales[4 * a :, stationary],
                rhs=codes[:].bitcast(FP8X4),
                rhs_scale=scales[:],
                start=start,
                stop=stop,
            )

        def e_pass(b, jh, mi):
            v2_pass(diff_banks[(mi, jh)], b, mi, packed[("h", b, jh)], False, b == 1)

        def y_tile(jh, mi):
            acc = bank("y_bank", [P, HALF])
            for a in range(2):
                v2_pass(acc, a, mi, packed[("wfix", a, jh)], a == 0, a == 1)
            tanh_y[(mi, jh)] = sbuf("tanh_y%d%d" % (mi, jh), [P, HALF], F32)
            nc.scalar.activation(tanh_y[(mi, jh)][:], acc[:], ACT.Tanh, scale=0.5)

        def gap_tile(jh, mi, cols=slice(0, HALF)):
            nc.scalar.activation(half_gap[(mi, jh)][:, cols], diff_banks[(mi, jh)][:, cols], ACT.Abs, scale=0.5)

        def finish_tile(jh, mi, cols=slice(0, HALF)):
            result = sbuf("result%d%d_%d" % (mi, jh, cols.start), [P, cols.stop - cols.start], F32)
            nc.vector.scalar_tensor_tensor(
                result[:], tanh_y[(mi, jh)][:, cols], 1.0, half_gap[(mi, jh)][:, cols], ALU.add, ALU.mult
            )
            nc.sync.dma_start(out[P * mi : P * (mi + 1), HALF * jh + cols.start : HALF * jh + cols.stop], result[:])

        nc.sync.dma_start(fillers[:], offs)
        load_table_words(0)
        load_table_scales()
        nc.sync.dma_start(suspects[:], offs2)
        load_weight("wdist", wdist, 0, 0)
        load_weight("wdist", wdist, 1, 0)
        load_table_words(1)
        load_weight("wdist", wdist, 0, 1)

        round_wdist(0, 0, [on_scalar, on_scalar])
        round_wdist(1, 0, [on_scalar, on_vector])
        round_wdist(0, 1, [on_scalar, on_vector])
        for jh in range(2):
            gather_v_words(0, jh)
            gather_v_scales(jh)

        load_weight("wdist", wdist, 1, 1)
        nc.sync.dma_start(skip_words[:].bitcast(I32), wskip_words.rearrange("a p c -> p a c").bitcast(I32))
        load_skip_scales()
        nc.sync.dma_start(v_scales_pass1[0:MOVED_ROWS, :].bitcast(I32), v_scales[4 : 4 + MOVED_ROWS, :].bitcast(I32))
        for jh in range(2):
            for a in range(2):
                load_weight("wfix", wfix, a, jh)

        quantise("wdist", 0, 0)
        for jh in range(2):
            h_pass(0, 0, jh)
        quantise("wdist", 1, 0)
        gather_v_words(1, 0, PIECE)
        gather_v_words(1, 1)
        gather_v2_words(0)
        quantise("wdist", 0, 1)
        round_wdist(1, 1, [on_vector, on_vector])
        h_abs_b0 = sbuf("h_abs_b0", [P, 2 * PACK * HALF], BF16, on="wdist_raw01")
        for jh in range(2):
            h_abs[(0, jh)] = h_abs_b0[:, PACK * HALF * jh : PACK * HALF * (jh + 1)]
        h_pass(1, 0, 0)
        quantise("wdist", 1, 1)
        h_pass(1, 0, 1)
        nc.vector.tensor_copy(v2_scales[:], table_scales[:].indirect(suspects[:]))

        h_abs[(1, 0)] = sbuf("h_abs10", [P, PACK * HALF], BF16)
        for a in range(2):
            h_pass(a, 1, 0)
        for a in range(2):
            for mi in range(M_TILES):
                f_pass(a, 0, mi)
        h_neg_b0 = sbuf("h_neg_b0", [P, 2 * PACK * HALF], BF16, on="wdist_raw11")
        for jh in range(2):
            grouped[("h", 0, jh)] = h_neg_b0[:, PACK * HALF * jh : PACK * HALF * (jh + 1)]
        negate_h(0, 0)
        quantise("h", 0, 0)
        gather_v2_words(1, on="wdist_bf11")
        h_abs[(1, 1)] = sbuf("h_abs11", [P, PACK * HALF], BF16, on="wfix_raw10")
        for n in range(4):
            for a in range(2):
                h_pass(a, 1, 1, [n])
        for mi in range(M_TILES):
            e_pass(0, 0, mi)
        grouped[("h", 1, 0)] = sbuf("h_neg10", [P, PACK * HALF], BF16)
        negate_h(1, 0)
        quantise("h", 1, 0)
        for mi in range(M_TILES):
            e_pass(1, 0, mi)

        round_wfix(0, 0, on_vector)
        quantise("wfix", 0, 0)
        round_wfix(1, 0, on_scalar)
        quantise("wfix", 1, 0)
        grouped[("h", 1, 1)] = sbuf("h_neg11", [P, PACK * HALF], BF16)
        for b in range(2):
            negate_h(b, 1)
            quantise("h", b, 1)
        for a in range(2):
            round_wfix(a, 1, on_vector)
            quantise("wfix", a, 1)

        half_gap_j0 = sbuf("half_gap_j0", [P, M_TILES * HALF], F32, on="wfix_bf10")
        for mi in range(M_TILES):
            half_gap[(mi, 0)] = half_gap_j0[:, HALF * mi : HALF * (mi + 1)]
            gap_tile(0, mi)
        for mi in range(M_TILES):
            y_tile(0, mi)
        for mi in range(M_TILES):
            finish_tile(0, mi)

        for mi in range(M_TILES):
            y_tile(1, mi)
            for a in range(2):
                f_pass(a, 1, mi)
            for b in range(2):
                e_pass(b, 1, mi)
            half_gap[(mi, 1)] = sbuf("half_gap%d1" % mi, [P, HALF], F32)
            width = PIECE if mi == M_TILES - 1 else HALF
            for c0 in range(0, HALF, width):
                gap_tile(1, mi, slice(c0, c0 + width))
                finish_tile(1, mi, slice(c0, c0 + width))
